import numpy as np, ml_dtypes
CORES = [44,45,46,47,172,173,174,175,300,301,302,303,428,429,430,431]
N = 16
DEG, TK, TIMES = 3, 512, 3
MASK = [[15,0,1],[0,1,2],[1,2,3],[2,3,4],[3,4,5],[4,5,6],[5,6,7],[6,7,8],[7,8,9],[8,9,10],[9,10,11],[10,11,12],[11,12,13],[12,13,14],[13,14,15],[14,15,0]]
def setup_inputs(rng):
    return {"x": rng.standard_normal((N, 128, TK), dtype=np.float32).astype(ml_dtypes.bfloat16), "w": (rng.standard_normal((N, 128, DEG * 128), dtype=np.float32) / np.float32(np.sqrt(128 * DEG / 2))).astype(ml_dtypes.bfloat16)}
def setup_inputs_big(rng):
    d = setup_inputs(rng)
    for k in ("x",): d[k] = (d[k].astype(np.float32) * 1048576.0).astype(d[k].dtype)
    return d
def setup_inputs_small(rng):
    d = setup_inputs(rng)
    for k in ("x",): d[k] = (d[k].astype(np.float32) * (1 / 1048576.0)).astype(d[k].dtype)
    return d
def setup_inputs_apart(rng):
    d = setup_inputs(rng)
    f = (10.0 ** rng.permutation(np.linspace(-1.5, 1.5, N))).astype(np.float32).reshape(N, 1, 1)
    for k in ("x",): d[k] = (d[k].astype(np.float32) * f).astype(d[k].dtype)
    return d
def reference(x, w):
    X, W = x.astype(np.float64), w.astype(np.float64)
    h = list(X)
    for _ in range(TIMES):
        h = [sum(W[r][:, 128 * i:128 * i + 128].T @ h[j] for i, j in enumerate(MASK[r])) for r in range(N)]
    return {"y": np.stack(h).astype(ml_dtypes.bfloat16)}

@@ -1,0 +1,112 @@
+from concourse.bass import DstId, RemoteDMATransfer
+
+P, TK, DEG, TIMES = 128, 512, 3, 3
+NCH = 2
+KE = 8
+CW = TK // NCH
+NBANK = min(8, TIMES * NCH)
+
+SCRATCH = {"w_sb": ("sbuf", [P, DEG * P], "bfloat16"), "yo": ("sbuf", [P, TK], "bfloat16")}
+for _s in range(TIMES):
+    SCRATCH["h%d" % _s] = ("sbuf", [P, DEG * TK], "bfloat16")
+for _b in range(NBANK):
+    SCRATCH["ps%d" % _b] = ("psum", [P, 512], "float32")
+
+SEMAPHORES = (["wl", "sent"]
+              + ["a%d_%d_%d" % (s, i, c) for s in range(TIMES) for i in range(DEG) for c in range(NCH)]
+              + ["m%d_%d" % (s, c) for s in range(TIMES) for c in range(NCH)]
+              + ["f%d" % c for c in range(NCH)] + ["st%d" % c for c in range(NCH)])
+
+
+def _pick(avail, k, used):
+    m, n = 0, 0
+    for b in range(avail.bit_length()):
+        bit = 1 << b
+        if n < k and (avail & bit) and not (used & bit):
+            m |= bit
+            n += 1
+    assert n == k
+    return m
+
+
+def rank_program(g, core, T, topo):
+    r = T.rank_of(core)
+    if r is None:
+        return
+    mask_t = T.tables["MASK"]
+    cores = T.cores
+
+    def one_chip(a, b):
+        return (topo.host(a), topo.chip(a)) == (topo.host(b), topo.chip(b))
+
+    def far_inputs(j):
+        return any(not one_chip(cores[k], cores[j]) for k in mask_t[j])
+
+    own = mask_t[r].index(r)
+    others = sorted((i for i in range(DEG) if i != own),
+                    key=lambda i: (not one_chip(cores[mask_t[r][i]], core), far_inputs(mask_t[r][i])))
+    cons = [(cores[q], i) for q in range(len(cores)) for i in range(DEG) if mask_t[q][i] == r and q != r]
+    cons.sort(key=lambda d: bin(topo.mask(core, d[0])).count("1"))
+    plan, used = [], 0
+    for d, i in cons:
+        assert topo.may_write(core, d)
+        em = _pick(topo.mask(core, d), KE, used)
+        used |= em
+        rid, pid = topo.addr(d, core)
+        plan.append((DstId(rid=rid, pnc=pid), em, i))
+
+    def col(i, c):
+        return slice(i * TK + c * CW, i * TK + (c + 1) * CW)
+
+    def avail(s, i, c):
+        return T.sem["a%d_%d_%d" % (s, i, c)]
+
+    def full(s, i):
+        return KE if i != own else (16 if s == 0 else 1)
+
+    ldq = [g.sync, g.scalar]
+
+    for c in range(NCH):
+        ldq[c % 2].dma_start(T.h0[:, col(own, c)], T.x[:, c * CW:(c + 1) * CW]).then_inc(avail(0, own, c), 16)
+    ldq[NCH % 2].dma_start(T.w_sb[:], T.w[:]).then_inc(T.sem.wl, 16)
+
+    for s in range(TIMES):
+        h = T["h%d" % s]
+        for c in range(NCH):
+            g.wait_ge(avail(s, own, c), full(s, own))
+            g.remote_dma_fused(
+                [RemoteDMATransfer(dst_ids=[did], dma_engine_mask=em, remote_sem=avail(s, i, c),
+                                   src=h[:, col(own, c)], dst=h[:, col(i, c)]) for did, em, i in plan],
+                local_sem=T.sem.sent)
+    g.wait_ge(T.sem.sent, TIMES * NCH * KE * len(plan))
+
+    g.tensor.wait_ge(T.sem.wl, 16)
+    for s in range(TIMES):
+        h = T["h%d" % s]
+        for c in range(NCH):
+            ps = T["ps%d" % ((s * NCH + c) % NBANK)]
+            g.tensor.wait_ge(avail(s, own, c), full(s, own))
+            g.tensor.matmul(ps[:, 0:CW], T.w_sb[:, own * P:(own + 1) * P], h[:, col(own, c)], start=True, stop=False)
+        for c in range(NCH):
+            ps = T["ps%d" % ((s * NCH + c) % NBANK)]
+            for n, i in enumerate(others):
+                g.tensor.wait_ge(avail(s, i, c), full(s, i))
+                mm = g.tensor.matmul(ps[:, 0:CW], T.w_sb[:, i * P:(i + 1) * P], h[:, col(i, c)],
+                                     start=False, stop=(n == len(others) - 1))
+            mm.then_inc(T.sem["m%d_%d" % (s, c)], 1)
+
+    for s in range(TIMES):
+        for c in range(NCH):
+            ps = T["ps%d" % ((s * NCH + c) % NBANK)]
+            g.vector.wait_ge(T.sem["m%d_%d" % (s, c)], 1)
+            if s + 1 < TIMES:
+                g.vector.tensor_copy(T["h%d" % (s + 1)][:, col(own, c)], ps[:, 0:CW]).then_inc(avail(s + 1, own, c), 1)
+            else:
+                g.vector.tensor_copy(T.yo[:, c * CW:(c + 1) * CW], ps[:, 0:CW]).then_inc(T.sem["f%d" % c], 1)
+
+    for c in range(NCH):
+        q = ldq[c % 2]
+        q.wait_ge(T.sem["f%d" % c], 1)
+        q.dma_start(T.y[:, c * CW:(c + 1) * CW], T.yo[:, c * CW:(c + 1) * CW]).then_inc(T.sem["st%d" % c], 16)
+    for c in range(NCH):
+        ldq[c % 2].wait_ge(T.sem["st%d" % c], 16)

@@ -1,26 +1,27 @@
 from concourse.bass import DstId, RemoteDMATransfer
 
 P, TK, DEG, TIMES = 128, 512, 3, 3
-NCH = 2
-KE = 8
-CW = TK // NCH
-NBANK = min(8, TIMES * NCH)
+SPLIT = 256
+BLK = [(0, SPLIT // 2), (SPLIT // 2, SPLIT), (SPLIT, (SPLIT + TK) // 2), ((SPLIT + TK) // 2, TK)]
+PART_B, PART_A = [0, 1], [2, 3]
+LAST = [0, 2, 1, 3]
 
 SCRATCH = {"w_sb": ("sbuf", [P, DEG * P], "bfloat16"), "yo": ("sbuf", [P, TK], "bfloat16")}
 for _s in range(TIMES):
     SCRATCH["h%d" % _s] = ("sbuf", [P, DEG * TK], "bfloat16")
-for _b in range(NBANK):
+for _b in range(8):
     SCRATCH["ps%d" % _b] = ("psum", [P, 512], "float32")
 
 SEMAPHORES = (["wl", "sent"]
-              + ["a%d_%d_%d" % (s, i, c) for s in range(TIMES) for i in range(DEG) for c in range(NCH)]
-              + ["m%d_%d" % (s, c) for s in range(TIMES) for c in range(NCH)]
-              + ["f%d" % c for c in range(NCH)] + ["st%d" % c for c in range(NCH)])
+              + ["a%d_%d_%d" % (s, i, c) for s in range(TIMES) for i in range(DEG) for c in range(4)]
+              + ["m%d_%d" % (s, c) for s in range(TIMES) for c in range(4)]
+              + ["f%d" % c for c in range(4)] + ["st%d" % c for c in range(4)])
 
 
-def _pick(avail, k, used):
+def _pick(avail, k, used, high=False):
     m, n = 0, 0
-    for b in range(avail.bit_length()):
+    bits = range(avail.bit_length())
+    for b in (reversed(bits) if high else bits):
         bit = 1 << b
         if n < k and (avail & bit) and not (used & bit):
             m |= bit
@@ -30,83 +31,139 @@ def _pick(avail, k, used):
 
 
 def rank_program(g, core, T, topo):
-    r = T.rank_of(core)
-    if r is None:
-        return
     mask_t = T.tables["MASK"]
     cores = T.cores
+    nr = len(cores)
 
     def one_chip(a, b):
         return (topo.host(a), topo.chip(a)) == (topo.host(b), topo.chip(b))
 
-    def far_inputs(j):
-        return any(not one_chip(cores[k], cores[j]) for k in mask_t[j])
+    def twin_of(q):
+        c0 = cores[q]
+        near = [c for c in range(max(0, c0 - 32), c0 + 32) if one_chip(c, c0)]
+        idle = [c for c in near if topo.die(c) != topo.die(c0) and T.rank_of(c) is None]
+        return idle[[c for c in near if T.rank_of(c) is not None].index(c0)]
+
+    twins = [twin_of(q) for q in range(nr)]
+    r = T.rank_of(core)
+    is_twin = r is None
+    if is_twin:
+        if core not in twins:
+            return
+        r = twins.index(core)
+
+    def n_eng(src, dst, nd):
+        return 8 if (nd <= 2 or not one_chip(src, dst)) else 4
+
+    def plan(cons):
+        cons = sorted(cons, key=lambda d: bin(topo.mask(core, d[0])).count("1"))
+        out, used = [], 0
+        for d, i in cons:
+            assert topo.may_write(core, d)
+            em = _pick(topo.mask(core, d), n_eng(core, d, len(cons)), used)
+            used |= em
+            rid, pid = topo.addr(d, core)
+            out.append((DstId(rid=rid, pnc=pid), em, i))
+        return out
 
     own = mask_t[r].index(r)
-    others = sorted((i for i in range(DEG) if i != own),
-                    key=lambda i: (not one_chip(cores[mask_t[r][i]], core), far_inputs(mask_t[r][i])))
-    cons = [(cores[q], i) for q in range(len(cores)) for i in range(DEG) if mask_t[q][i] == r and q != r]
-    cons.sort(key=lambda d: bin(topo.mask(core, d[0])).count("1"))
-    plan, used = [], 0
-    for d, i in cons:
-        assert topo.may_write(core, d)
-        em = _pick(topo.mask(core, d), KE, used)
-        used |= em
-        rid, pid = topo.addr(d, core)
-        plan.append((DstId(rid=rid, pnc=pid), em, i))
+    users = [q for q in range(nr) if q != r and r in mask_t[q]]
+    far = lambda j: any(not one_chip(cores[k], cores[j]) for k in mask_t[j])
+    order = sorted(range(DEG), key=lambda i: (not one_chip(cores[mask_t[r][i]], core), far(mask_t[r][i])))
+    others = [i for i in order if i != own]
 
-    def col(i, c):
-        return slice(i * TK + c * CW, i * TK + (c + 1) * CW)
+    sem = T.sem
+    a_sem = lambda s, i, c: sem["a%d_%d_%d" % (s, i, c)]
+    col = lambda i, c0, c1: slice(i * TK + c0, i * TK + c1)
+    blk = lambda i, c: col(i, BLK[c][0], BLK[c][1])
+    tile = lambda i: slice(i * P, (i + 1) * P)
+    bank = lambda s, c: T["ps%d" % (2 * s + c % 2 if s < 2 else 4 + c)]
+    wid = lambda c: BLK[c][1] - BLK[c][0]
+    te, ve = g.tensor, g.vector
+    sent = [0]
 
-    def avail(s, i, c):
-        return T.sem["a%d_%d_%d" % (s, i, c)]
+    def send(h, c0, c1, pl, s, c):
+        g.remote_dma_fused(
+            [RemoteDMATransfer(dst_ids=[did], dma_engine_mask=em, remote_sem=a_sem(s, i, c),
+                               src=h[:, col(own, c0, c1)], dst=h[:, col(i, c0, c1)]) for did, em, i in pl],
+            local_sem=sem.sent)
+        sent[0] += sum(bin(em).count("1") for _, em, _ in pl)
 
-    def full(s, i):
-        return KE if i != own else (16 if s == 0 else 1)
-
-    ldq = [g.sync, g.scalar]
-
-    for c in range(NCH):
-        ldq[c % 2].dma_start(T.h0[:, col(own, c)], T.x[:, c * CW:(c + 1) * CW]).then_inc(avail(0, own, c), 16)
-    ldq[NCH % 2].dma_start(T.w_sb[:], T.w[:]).then_inc(T.sem.wl, 16)
-
-    for s in range(TIMES):
+    def group(s, c, slots, sems, first, last):
         h = T["h%d" % s]
-        for c in range(NCH):
-            g.wait_ge(avail(s, own, c), full(s, own))
-            g.remote_dma_fused(
-                [RemoteDMATransfer(dst_ids=[did], dma_engine_mask=em, remote_sem=avail(s, i, c),
-                                   src=h[:, col(own, c)], dst=h[:, col(i, c)]) for did, em, i in plan],
-                local_sem=T.sem.sent)
-    g.wait_ge(T.sem.sent, TIMES * NCH * KE * len(plan))
+        for n, i in enumerate(slots):
+            te.wait_ge(sems[n][0], sems[n][1])
+            mm = te.matmul(bank(s, c)[:, 0:wid(c)], T.w_sb[:, tile(i)], h[:, blk(i, c)],
+                           start=(first and n == 0), stop=(last and n == len(slots) - 1))
+        return mm
 
-    g.tensor.wait_ge(T.sem.wl, 16)
-    for s in range(TIMES):
-        h = T["h%d" % s]
-        for c in range(NCH):
-            ps = T["ps%d" % ((s * NCH + c) % NBANK)]
-            g.tensor.wait_ge(avail(s, own, c), full(s, own))
-            g.tensor.matmul(ps[:, 0:CW], T.w_sb[:, own * P:(own + 1) * P], h[:, col(own, c)], start=True, stop=False)
-        for c in range(NCH):
-            ps = T["ps%d" % ((s * NCH + c) % NBANK)]
-            for n, i in enumerate(others):
-                g.tensor.wait_ge(avail(s, i, c), full(s, i))
-                mm = g.tensor.matmul(ps[:, 0:CW], T.w_sb[:, i * P:(i + 1) * P], h[:, col(i, c)],
-                                     start=False, stop=(n == len(others) - 1))
-            mm.then_inc(T.sem["m%d_%d" % (s, c)], 1)
+    part = PART_B if is_twin else PART_A
 
-    for s in range(TIMES):
-        for c in range(NCH):
-            ps = T["ps%d" % ((s * NCH + c) % NBANK)]
-            g.vector.wait_ge(T.sem["m%d_%d" % (s, c)], 1)
-            if s + 1 < TIMES:
-                g.vector.tensor_copy(T["h%d" % (s + 1)][:, col(own, c)], ps[:, 0:CW]).then_inc(avail(s + 1, own, c), 1)
+    if is_twin:
+        to_twins = plan([(twins[q], mask_t[q].index(r)) for q in users])
+        home = plan([(cores[q], mask_t[q].index(r)) for q in users + [r]])
+        for c in part:
+            g.wait_ge(a_sem(1, own, c), 1)
+            send(T.h1, BLK[c][0], BLK[c][1], to_twins, 1, c)
+        for c in part:
+            g.wait_ge(a_sem(2, own, c), 1)
+            send(T.h2, BLK[c][0], BLK[c][1], home, 2, c)
+        g.wait_ge(sem.sent, sent[0])
+        te.wait_ge(sem.wl, 8)
+    else:
+        to_ranks = plan([(cores[q], mask_t[q].index(r)) for q in users])
+        g.sync.dma_start(T.h0[:, col(own, 0, SPLIT)], T.x[:, 0:SPLIT]).then_inc(a_sem(0, own, 0), 16)
+        g.scalar.dma_start(T.w_sb[:], T.w[:]).then_inc(sem.wl, 16)
+        g.sync.dma_start(T.h0[:, col(own, SPLIT, TK)], T.x[:, SPLIT:TK]).then_inc(a_sem(0, own, 2), 16)
+        g.wait_ge(a_sem(0, own, 0), 16)
+        send(T.h0, 0, SPLIT, plan([(twins[q], mask_t[q].index(r)) for q in users + [r]]), 0, 0)
+        g.wait_ge(sem.wl, 16)
+        rid, pid = topo.addr(twins[r], core)
+        g.remote_dma(T.w_sb[:], T.w_sb[:], sem.wl, sem.sent, pid, rid, _pick(topo.mask(core, twins[r]), 8, 0, high=True))
+        sent[0] += 8
+        g.wait_ge(a_sem(0, own, 2), 16)
+        send(T.h0, SPLIT, TK, to_ranks, 0, 2)
+        for s in (1, 2):
+            for c in part:
+                g.wait_ge(a_sem(s, own, c), 1)
+                send(T["h%d" % s], BLK[c][0], BLK[c][1], to_ranks, s, c)
+        g.wait_ge(sem.sent, sent[0])
+        te.wait_ge(sem.wl, 16)
+
+    if is_twin:
+        for c in part:
+            group(0, c, order, [(a_sem(0, i, 0), n_eng(cores[mask_t[r][i]], core, 3)) for i in order], True, True
+                  ).then_inc(sem["m0_%d" % c], 1)
+    else:
+        for c in part:
+            group(0, c, [own], [(a_sem(0, own, 2), 16)], True, False)
+        for c in part:
+            group(0, c, others, [(a_sem(0, i, 2), 8) for i in others], False, True).then_inc(sem["m0_%d" % c], 1)
+    for c in part:
+        group(1, c, [own], [(a_sem(1, own, c), 1)], True, False)
+    for c in part:
+        group(1, c, others, [(a_sem(1, i, c), 8) for i in others], False, True).then_inc(sem["m1_%d" % c], 1)
+    if not is_twin:
+        for c in part:
+            group(2, c, [own], [(a_sem(2, own, c), 1)], True, False)
+        for c in LAST:
+            if c in part:
+                mm = group(2, c, others, [(a_sem(2, i, c), 8) for i in others], False, True)
             else:
-                g.vector.tensor_copy(T.yo[:, c * CW:(c + 1) * CW], ps[:, 0:CW]).then_inc(T.sem["f%d" % c], 1)
+                mm = group(2, c, order, [(a_sem(2, i, c), n_eng(twins[mask_t[r][i]], core, 3)) for i in order], True, True)
+            mm.then_inc(sem["m2_%d" % c], 1)
 
-    for c in range(NCH):
-        q = ldq[c % 2]
-        q.wait_ge(T.sem["f%d" % c], 1)
-        q.dma_start(T.y[:, c * CW:(c + 1) * CW], T.yo[:, c * CW:(c + 1) * CW]).then_inc(T.sem["st%d" % c], 16)
-    for c in range(NCH):
-        ldq[c % 2].wait_ge(T.sem["st%d" % c], 16)
+    for s in (0, 1):
+        for c in part:
+            ve.wait_ge(sem["m%d_%d" % (s, c)], 1)
+            ve.tensor_copy(T["h%d" % (s + 1)][:, blk(own, c)], bank(s, c)[:, 0:wid(c)]).then_inc(a_sem(s + 1, own, c), 1)
+    if not is_twin:
+        for c in LAST:
+            ve.wait_ge(sem["m2_%d" % c], 1)
+            ve.tensor_copy(T.yo[:, BLK[c][0]:BLK[c][1]], bank(2, c)[:, 0:wid(c)]).then_inc(sem["f%d" % c], 1)
+        qs = [g.sync, g.scalar]
+        for n, c in enumerate(LAST):
+            qs[n % 2].wait_ge(sem["f%d" % c], 1)
+            qs[n % 2].dma_start(T.y[:, BLK[c][0]:BLK[c][1]], T.yo[:, BLK[c][0]:BLK[c][1]]).then_inc(sem["st%d" % c], 16)
+        for n, c in enumerate(LAST):
+            qs[n % 2].wait_ge(sem["st%d" % c], 16)

@@ -2,7 +2,8 @@ from concourse.bass import DstId, RemoteDMATransfer
 
 P, TK, DEG, TIMES = 128, 512, 3, 3
 SPLIT = 256
-BLK = [(0, SPLIT // 2), (SPLIT // 2, SPLIT), (SPLIT, (SPLIT + TK) // 2), ((SPLIT + TK) // 2, TK)]
+LEAD = 152
+BLK = [(0, LEAD), (LEAD, SPLIT), (SPLIT, SPLIT + LEAD), (SPLIT + LEAD, TK)]
 PART_B, PART_A = [0, 1], [2, 3]
 LAST = [0, 2, 1, 3]
 
@@ -82,10 +83,11 @@ def rank_program(g, core, T, topo):
     te, ve = g.tensor, g.vector
     sent = [0]
 
-    def send(h, c0, c1, pl, s, c):
+    def send(s, c, pl):
+        h = T["h%d" % s]
         g.remote_dma_fused(
             [RemoteDMATransfer(dst_ids=[did], dma_engine_mask=em, remote_sem=a_sem(s, i, c),
-                               src=h[:, col(own, c0, c1)], dst=h[:, col(i, c0, c1)]) for did, em, i in pl],
+                               src=h[:, blk(own, c)], dst=h[:, blk(i, c)]) for did, em, i in pl],
             local_sem=sem.sent)
         sent[0] += sum(bin(em).count("1") for _, em, _ in pl)
 
@@ -104,41 +106,44 @@ def rank_program(g, core, T, topo):
         home = plan([(cores[q], mask_t[q].index(r)) for q in users + [r]])
         for c in part:
             g.wait_ge(a_sem(1, own, c), 1)
-            send(T.h1, BLK[c][0], BLK[c][1], to_twins, 1, c)
+            send(1, c, to_twins)
         for c in part:
             g.wait_ge(a_sem(2, own, c), 1)
-            send(T.h2, BLK[c][0], BLK[c][1], home, 2, c)
+            send(2, c, home)
         g.wait_ge(sem.sent, sent[0])
         te.wait_ge(sem.wl, 8)
     else:
         to_ranks = plan([(cores[q], mask_t[q].index(r)) for q in users])
+        x_to_twins = plan([(twins[q], mask_t[q].index(r)) for q in users + [r]])
         g.sync.dma_start(T.h0[:, col(own, 0, SPLIT)], T.x[:, 0:SPLIT]).then_inc(a_sem(0, own, 0), 16)
         g.scalar.dma_start(T.w_sb[:], T.w[:]).then_inc(sem.wl, 16)
         g.sync.dma_start(T.h0[:, col(own, SPLIT, TK)], T.x[:, SPLIT:TK]).then_inc(a_sem(0, own, 2), 16)
         g.wait_ge(a_sem(0, own, 0), 16)
-        send(T.h0, 0, SPLIT, plan([(twins[q], mask_t[q].index(r)) for q in users + [r]]), 0, 0)
+        for c in PART_B:
+            send(0, c, x_to_twins)
         g.wait_ge(sem.wl, 16)
         rid, pid = topo.addr(twins[r], core)
         g.remote_dma(T.w_sb[:], T.w_sb[:], sem.wl, sem.sent, pid, rid, _pick(topo.mask(core, twins[r]), 8, 0, high=True))
         sent[0] += 8
         g.wait_ge(a_sem(0, own, 2), 16)
-        send(T.h0, SPLIT, TK, to_ranks, 0, 2)
+        for c in PART_A:
+            send(0, c, to_ranks)
         for s in (1, 2):
             for c in part:
                 g.wait_ge(a_sem(s, own, c), 1)
-                send(T["h%d" % s], BLK[c][0], BLK[c][1], to_ranks, s, c)
+                send(s, c, to_ranks)
         g.wait_ge(sem.sent, sent[0])
         te.wait_ge(sem.wl, 16)
 
     if is_twin:
         for c in part:
-            group(0, c, order, [(a_sem(0, i, 0), n_eng(cores[mask_t[r][i]], core, 3)) for i in order], True, True
+            group(0, c, order, [(a_sem(0, i, c), n_eng(cores[mask_t[r][i]], core, 3)) for i in order], True, True
                   ).then_inc(sem["m0_%d" % c], 1)
     else:
         for c in part:
             group(0, c, [own], [(a_sem(0, own, 2), 16)], True, False)
         for c in part:
-            group(0, c, others, [(a_sem(0, i, 2), 8) for i in others], False, True).then_inc(sem["m0_%d" % c], 1)
+            group(0, c, others, [(a_sem(0, i, c), 8) for i in others], False, True).then_inc(sem["m0_%d" % c], 1)
     for c in part:
         group(1, c, [own], [(a_sem(1, own, c), 1)], True, False)
     for c in part:

@@ -1,11 +1,15 @@
 from concourse.bass import DstId, RemoteDMATransfer
 
 P, TK, DEG, TIMES = 128, 512, 3, 3
-SPLIT = 256
-LEAD = 152
-BLK = [(0, LEAD), (LEAD, SPLIT), (SPLIT, SPLIT + LEAD), (SPLIT + LEAD, TK)]
-PART_B, PART_A = [0, 1], [2, 3]
-LAST = [0, 2, 1, 3]
+WIDTHS = [120, 80, 56]
+NBK = len(WIDTHS)
+SPLIT = sum(WIDTHS)
+BLK = []
+for _p in range(2):
+    for _k in range(NBK):
+        BLK.append((_p * SPLIT + sum(WIDTHS[:_k]), _p * SPLIT + sum(WIDTHS[:_k + 1])))
+PART_B, PART_A = list(range(NBK)), list(range(NBK, 2 * NBK))
+LAST = [c for k in range(NBK) for c in (k, NBK + k)]
 
 SCRATCH = {"w_sb": ("sbuf", [P, DEG * P], "bfloat16"), "yo": ("sbuf", [P, TK], "bfloat16")}
 for _s in range(TIMES):
@@ -14,9 +18,9 @@ for _b in range(8):
     SCRATCH["ps%d" % _b] = ("psum", [P, 512], "float32")
 
 SEMAPHORES = (["wl", "sent"]
-              + ["a%d_%d_%d" % (s, i, c) for s in range(TIMES) for i in range(DEG) for c in range(4)]
-              + ["m%d_%d" % (s, c) for s in range(TIMES) for c in range(4)]
-              + ["f%d" % c for c in range(4)] + ["st%d" % c for c in range(4)])
+              + ["a%d_%d_%d" % (s, i, c) for s in range(TIMES) for i in range(DEG) for c in range(2 * NBK)]
+              + ["m%d_%d" % (s, c) for s in range(TIMES) for c in range(2 * NBK)]
+              + ["f%d" % c for c in range(2 * NBK)] + ["st%d" % c for c in range(2 * NBK)])
 
 
 def _pick(avail, k, used, high=False):
@@ -78,7 +82,7 @@ def rank_program(g, core, T, topo):
     col = lambda i, c0, c1: slice(i * TK + c0, i * TK + c1)
     blk = lambda i, c: col(i, BLK[c][0], BLK[c][1])
     tile = lambda i: slice(i * P, (i + 1) * P)
-    bank = lambda s, c: T["ps%d" % (2 * s + c % 2 if s < 2 else 4 + c)]
+    bank = lambda s, c: T["ps%d" % ((s * NBK + c % NBK if s < 2 else 2 * NBK + c) % 8)]
     wid = lambda c: BLK[c][1] - BLK[c][0]
     te, ve = g.tensor, g.vector
     sent = [0]
@@ -100,6 +104,7 @@ def rank_program(g, core, T, topo):
         return mm
 
     part = PART_B if is_twin else PART_A
+    ld_b, ld_a = a_sem(0, own, PART_B[0]), a_sem(0, own, PART_A[0])
 
     if is_twin:
         to_twins = plan([(twins[q], mask_t[q].index(r)) for q in users])
@@ -115,17 +120,19 @@ def rank_program(g, core, T, topo):
     else:
         to_ranks = plan([(cores[q], mask_t[q].index(r)) for q in users])
         x_to_twins = plan([(twins[q], mask_t[q].index(r)) for q in users + [r]])
-        g.sync.dma_start(T.h0[:, col(own, 0, SPLIT)], T.x[:, 0:SPLIT]).then_inc(a_sem(0, own, 0), 16)
+        g.sync.dma_start(T.h0[:, col(own, 0, SPLIT)], T.x[:, 0:SPLIT]).then_inc(ld_b, 16)
         g.scalar.dma_start(T.w_sb[:], T.w[:]).then_inc(sem.wl, 16)
-        g.sync.dma_start(T.h0[:, col(own, SPLIT, TK)], T.x[:, SPLIT:TK]).then_inc(a_sem(0, own, 2), 16)
-        g.wait_ge(a_sem(0, own, 0), 16)
+        g.sync.dma_start(T.h0[:, col(own, SPLIT, TK)], T.x[:, SPLIT:TK]).then_inc(ld_a, 16)
+        g.wait_ge(ld_b, 16)
         for c in PART_B:
             send(0, c, x_to_twins)
-        g.wait_ge(sem.wl, 16)
-        rid, pid = topo.addr(twins[r], core)
-        g.remote_dma(T.w_sb[:], T.w_sb[:], sem.wl, sem.sent, pid, rid, _pick(topo.mask(core, twins[r]), 8, 0, high=True))
-        sent[0] += 8
-        g.wait_ge(a_sem(0, own, 2), 16)
+            if c == PART_B[0]:
+                g.wait_ge(sem.wl, 16)
+                rid, pid = topo.addr(twins[r], core)
+                g.remote_dma(T.w_sb[:], T.w_sb[:], sem.wl, sem.sent, pid, rid,
+                             _pick(topo.mask(core, twins[r]), 8, 0, high=True))
+                sent[0] += 8
+        g.wait_ge(ld_a, 16)
         for c in PART_A:
             send(0, c, to_ranks)
         for s in (1, 2):
@@ -141,7 +148,7 @@ def rank_program(g, core, T, topo):
                   ).then_inc(sem["m0_%d" % c], 1)
     else:
         for c in part:
-            group(0, c, [own], [(a_sem(0, own, 2), 16)], True, False)
+            group(0, c, [own], [(ld_a, 16)], True, False)
         for c in part:
             group(0, c, others, [(a_sem(0, i, c), 8) for i in others], False, True).then_inc(sem["m0_%d" % c], 1)
     for c in part:

@@ -1,15 +1,18 @@
 from concourse.bass import DstId, RemoteDMATransfer
 
 P, TK, DEG, TIMES = 128, 512, 3, 3
-WIDTHS = [120, 80, 56]
-NBK = len(WIDTHS)
-SPLIT = sum(WIDTHS)
-BLK = []
-for _p in range(2):
-    for _k in range(NBK):
-        BLK.append((_p * SPLIT + sum(WIDTHS[:_k]), _p * SPLIT + sum(WIDTHS[:_k + 1])))
-PART_B, PART_A = list(range(NBK)), list(range(NBK, 2 * NBK))
-LAST = [c for k in range(NBK) for c in (k, NBK + k)]
+W_B = [88, 72, 72, 56]
+W_A = [104, 72, 48]
+SPLIT = sum(W_B)
+_E = [0]
+for _w in W_B + W_A:
+    _E.append(_E[-1] + _w)
+BLK = [(_E[_k], _E[_k + 1]) for _k in range(len(_E) - 1)]
+NBL = len(BLK)
+PART_B, PART_A = list(range(len(W_B))), list(range(len(W_B), NBL))
+RELAY = PART_B[2:]
+LAST = [0, 4, 1, 5, 2, 6, 3]
+BANK2 = {4: 6, 5: 7, 6: 0, 0: 1, 1: 2, 2: 3, 3: 4}
 
 SCRATCH = {"w_sb": ("sbuf", [P, DEG * P], "bfloat16"), "yo": ("sbuf", [P, TK], "bfloat16")}
 for _s in range(TIMES):
@@ -18,9 +21,9 @@ for _b in range(8):
     SCRATCH["ps%d" % _b] = ("psum", [P, 512], "float32")
 
 SEMAPHORES = (["wl", "sent"]
-              + ["a%d_%d_%d" % (s, i, c) for s in range(TIMES) for i in range(DEG) for c in range(2 * NBK)]
-              + ["m%d_%d" % (s, c) for s in range(TIMES) for c in range(2 * NBK)]
-              + ["f%d" % c for c in range(2 * NBK)] + ["st%d" % c for c in range(2 * NBK)])
+              + ["a%d_%d_%d" % (s, i, c) for s in range(TIMES) for i in range(DEG) for c in range(NBL)]
+              + ["m%d_%d" % (s, c) for s in range(TIMES) for c in range(NBL)]
+              + ["f%d" % c for c in range(NBL)] + ["st%d" % c for c in range(NBL)])
 
 
 def _pick(avail, k, used, high=False):
@@ -60,12 +63,12 @@ def rank_program(g, core, T, topo):
     def n_eng(src, dst, nd):
         return 8 if (nd <= 2 or not one_chip(src, dst)) else 4
 
-    def plan(cons):
+    def plan(cons, nd=None, used=0):
         cons = sorted(cons, key=lambda d: bin(topo.mask(core, d[0])).count("1"))
-        out, used = [], 0
+        out = []
         for d, i in cons:
             assert topo.may_write(core, d)
-            em = _pick(topo.mask(core, d), n_eng(core, d, len(cons)), used)
+            em = _pick(topo.mask(core, d), n_eng(core, d, nd or len(cons)), used)
             used |= em
             rid, pid = topo.addr(d, core)
             out.append((DstId(rid=rid, pnc=pid), em, i))
@@ -76,13 +79,14 @@ def rank_program(g, core, T, topo):
     far = lambda j: any(not one_chip(cores[k], cores[j]) for k in mask_t[j])
     order = sorted(range(DEG), key=lambda i: (not one_chip(cores[mask_t[r][i]], core), far(mask_t[r][i])))
     others = [i for i in order if i != own]
+    part = PART_B if is_twin else PART_A
 
     sem = T.sem
     a_sem = lambda s, i, c: sem["a%d_%d_%d" % (s, i, c)]
     col = lambda i, c0, c1: slice(i * TK + c0, i * TK + c1)
     blk = lambda i, c: col(i, BLK[c][0], BLK[c][1])
     tile = lambda i: slice(i * P, (i + 1) * P)
-    bank = lambda s, c: T["ps%d" % ((s * NBK + c % NBK if s < 2 else 2 * NBK + c) % 8)]
+    bank = lambda s, c: T["ps%d" % (s * len(part) + part.index(c) if s < 2 else BANK2[c])]
     wid = lambda c: BLK[c][1] - BLK[c][0]
     te, ve = g.tensor, g.vector
     sent = [0]
@@ -103,12 +107,16 @@ def rank_program(g, core, T, topo):
                            start=(first and n == 0), stop=(last and n == len(slots) - 1))
         return mm
 
-    part = PART_B if is_twin else PART_A
     ld_b, ld_a = a_sem(0, own, PART_B[0]), a_sem(0, own, PART_A[0])
 
     if is_twin:
         to_twins = plan([(twins[q], mask_t[q].index(r)) for q in users])
         home = plan([(cores[q], mask_t[q].index(r)) for q in users + [r]])
+        onward = plan([(twins[q], mask_t[q].index(r)) for q in users if not one_chip(twins[q], core)])
+        if onward:
+            for c in RELAY:
+                g.wait_ge(a_sem(0, own, c), n_eng(cores[r], core, 3))
+                send(0, c, onward)
         for c in part:
             g.wait_ge(a_sem(1, own, c), 1)
             send(1, c, to_twins)
@@ -120,12 +128,17 @@ def rank_program(g, core, T, topo):
     else:
         to_ranks = plan([(cores[q], mask_t[q].index(r)) for q in users])
         x_to_twins = plan([(twins[q], mask_t[q].index(r)) for q in users + [r]])
+        keep = 0
+        for q in users:
+            if not one_chip(twins[q], core):
+                keep |= topo.mask(core, twins[q])
+        x_near = plan([(twins[q], mask_t[q].index(r)) for q in users + [r] if one_chip(twins[q], core)], 3, keep)
         g.sync.dma_start(T.h0[:, col(own, 0, SPLIT)], T.x[:, 0:SPLIT]).then_inc(ld_b, 16)
         g.scalar.dma_start(T.w_sb[:], T.w[:]).then_inc(sem.wl, 16)
         g.sync.dma_start(T.h0[:, col(own, SPLIT, TK)], T.x[:, SPLIT:TK]).then_inc(ld_a, 16)
         g.wait_ge(ld_b, 16)
-        for c in PART_B:
-            send(0, c, x_to_twins)
+        for c in [RELAY[0], PART_B[0], RELAY[1], PART_B[1]]:
+            send(0, c, x_near if c in RELAY else x_to_twins)
             if c == PART_B[0]:
                 g.wait_ge(sem.wl, 16)
                 rid, pid = topo.addr(twins[r], core)

from concourse.bass import DstId, RemoteDMATransfer

P, TK, DEG, TIMES = 128, 512, 3, 3
W_B = [88, 72, 72, 56]
W_A = [104, 72, 48]
SPLIT = sum(W_B)
_E = [0]
for _w in W_B + W_A:
    _E.append(_E[-1] + _w)
BLK = [(_E[_k], _E[_k + 1]) for _k in range(len(_E) - 1)]
NBL = len(BLK)
PART_B, PART_A = list(range(len(W_B))), list(range(len(W_B), NBL))
RELAY = PART_B[2:]
LAST = [0, 4, 1, 5, 2, 6, 3]
BANK2 = {4: 6, 5: 7, 6: 0, 0: 1, 1: 2, 2: 3, 3: 4}

SCRATCH = {"w_sb": ("sbuf", [P, DEG * P], "bfloat16"), "yo": ("sbuf", [P, TK], "bfloat16")}
for _s in range(TIMES):
    SCRATCH["h%d" % _s] = ("sbuf", [P, DEG * TK], "bfloat16")
for _b in range(8):
    SCRATCH["ps%d" % _b] = ("psum", [P, 512], "float32")

SEMAPHORES = (["wl", "sent"]
              + ["a%d_%d_%d" % (s, i, c) for s in range(TIMES) for i in range(DEG) for c in range(NBL)]
              + ["m%d_%d" % (s, c) for s in range(TIMES) for c in range(NBL)]
              + ["f%d" % c for c in range(NBL)] + ["st%d" % c for c in range(NBL)])


def _pick(avail, k, used, high=False):
    m, n = 0, 0
    bits = range(avail.bit_length())
    for b in (reversed(bits) if high else bits):
        bit = 1 << b
        if n < k and (avail & bit) and not (used & bit):
            m |= bit
            n += 1
    assert n == k
    return m


def rank_program(g, core, T, topo):
    mask_t = T.tables["MASK"]
    cores = T.cores
    nr = len(cores)

    def one_chip(a, b):
        return (topo.host(a), topo.chip(a)) == (topo.host(b), topo.chip(b))

    def twin_of(q):
        c0 = cores[q]
        near = [c for c in range(max(0, c0 - 32), c0 + 32) if one_chip(c, c0)]
        idle = [c for c in near if topo.die(c) != topo.die(c0) and T.rank_of(c) is None]
        return idle[[c for c in near if T.rank_of(c) is not None].index(c0)]

    twins = [twin_of(q) for q in range(nr)]
    r = T.rank_of(core)
    is_twin = r is None
    if is_twin:
        if core not in twins:
            return
        r = twins.index(core)

    def n_eng(src, dst, nd):
        return 8 if (nd <= 2 or not one_chip(src, dst)) else 4

    def plan(cons, nd=None, used=0):
        cons = sorted(cons, key=lambda d: bin(topo.mask(core, d[0])).count("1"))
        out = []
        for d, i in cons:
            assert topo.may_write(core, d)
            em = _pick(topo.mask(core, d), n_eng(core, d, nd or len(cons)), used)
            used |= em
            rid, pid = topo.addr(d, core)
            out.append((DstId(rid=rid, pnc=pid), em, i))
        return out

    own = mask_t[r].index(r)
    users = [q for q in range(nr) if q != r and r in mask_t[q]]
    far = lambda j: any(not one_chip(cores[k], cores[j]) for k in mask_t[j])
    order = sorted(range(DEG), key=lambda i: (not one_chip(cores[mask_t[r][i]], core), far(mask_t[r][i])))
    others = [i for i in order if i != own]
    part = PART_B if is_twin else PART_A

    sem = T.sem
    a_sem = lambda s, i, c: sem["a%d_%d_%d" % (s, i, c)]
    col = lambda i, c0, c1: slice(i * TK + c0, i * TK + c1)
    blk = lambda i, c: col(i, BLK[c][0], BLK[c][1])
    tile = lambda i: slice(i * P, (i + 1) * P)
    bank = lambda s, c: T["ps%d" % (s * len(part) + part.index(c) if s < 2 else BANK2[c])]
    wid = lambda c: BLK[c][1] - BLK[c][0]
    te, ve = g.tensor, g.vector
    sent = [0]

    def send(s, c, pl):
        h = T["h%d" % s]
        g.remote_dma_fused(
            [RemoteDMATransfer(dst_ids=[did], dma_engine_mask=em, remote_sem=a_sem(s, i, c),
                               src=h[:, blk(own, c)], dst=h[:, blk(i, c)]) for did, em, i in pl],
            local_sem=sem.sent)
        sent[0] += sum(bin(em).count("1") for _, em, _ in pl)

    def group(s, c, slots, sems, first, last):
        h = T["h%d" % s]
        for n, i in enumerate(slots):
            te.wait_ge(sems[n][0], sems[n][1])
            mm = te.matmul(bank(s, c)[:, 0:wid(c)], T.w_sb[:, tile(i)], h[:, blk(i, c)],
                           start=(first and n == 0), stop=(last and n == len(slots) - 1))
        return mm

    ld_b, ld_a = a_sem(0, own, PART_B[0]), a_sem(0, own, PART_A[0])

    if is_twin:
        to_twins = plan([(twins[q], mask_t[q].index(r)) for q in users])
        home = plan([(cores[q], mask_t[q].index(r)) for q in users + [r]])
        onward = plan([(twins[q], mask_t[q].index(r)) for q in users if not one_chip(twins[q], core)])
        if onward:
            for c in RELAY:
                g.wait_ge(a_sem(0, own, c), n_eng(cores[r], core, 3))
                send(0, c, onward)
        for c in part:
            g.wait_ge(a_sem(1, own, c), 1)
            send(1, c, to_twins)
        for c in part:
            g.wait_ge(a_sem(2, own, c), 1)
            send(2, c, home)
        g.wait_ge(sem.sent, sent[0])
        te.wait_ge(sem.wl, 8)
    else:
        to_ranks = plan([(cores[q], mask_t[q].index(r)) for q in users])
        x_to_twins = plan([(twins[q], mask_t[q].index(r)) for q in users + [r]])
        keep = 0
        for q in users:
            if not one_chip(twins[q], core):
                keep |= topo.mask(core, twins[q])
        x_near = plan([(twins[q], mask_t[q].index(r)) for q in users + [r] if one_chip(twins[q], core)], 3, keep)
        g.sync.dma_start(T.h0[:, col(own, 0, SPLIT)], T.x[:, 0:SPLIT]).then_inc(ld_b, 16)
        g.scalar.dma_start(T.w_sb[:], T.w[:]).then_inc(sem.wl, 16)
        g.sync.dma_start(T.h0[:, col(own, SPLIT, TK)], T.x[:, SPLIT:TK]).then_inc(ld_a, 16)
        g.wait_ge(ld_b, 16)
        for c in [RELAY[0], PART_B[0], RELAY[1], PART_B[1]]:
            send(0, c, x_near if c in RELAY else x_to_twins)
            if c == PART_B[0]:
                g.wait_ge(sem.wl, 16)
                rid, pid = topo.addr(twins[r], core)
                g.remote_dma(T.w_sb[:], T.w_sb[:], sem.wl, sem.sent, pid, rid,
                             _pick(topo.mask(core, twins[r]), 8, 0, high=True))
                sent[0] += 8
        g.wait_ge(ld_a, 16)
        for c in PART_A:
            send(0, c, to_ranks)
        for s in (1, 2):
            for c in part:
                g.wait_ge(a_sem(s, own, c), 1)
                send(s, c, to_ranks)
        g.wait_ge(sem.sent, sent[0])
        te.wait_ge(sem.wl, 16)

    if is_twin:
        for c in part:
            group(0, c, order, [(a_sem(0, i, c), n_eng(cores[mask_t[r][i]], core, 3)) for i in order], True, True
                  ).then_inc(sem["m0_%d" % c], 1)
    else:
        for c in part:
            group(0, c, [own], [(ld_a, 16)], True, False)
        for c in part:
            group(0, c, others, [(a_sem(0, i, c), 8) for i in others], False, True).then_inc(sem["m0_%d" % c], 1)
    for c in part:
        group(1, c, [own], [(a_sem(1, own, c), 1)], True, False)
    for c in part:
        group(1, c, others, [(a_sem(1, i, c), 8) for i in others], False, True).then_inc(sem["m1_%d" % c], 1)
    if not is_twin:
        for c in part:
            group(2, c, [own], [(a_sem(2, own, c), 1)], True, False)
        for c in LAST:
            if c in part:
                mm = group(2, c, others, [(a_sem(2, i, c), 8) for i in others], False, True)
            else:
                mm = group(2, c, order, [(a_sem(2, i, c), n_eng(twins[mask_t[r][i]], core, 3)) for i in order], True, True)
            mm.then_inc(sem["m2_%d" % c], 1)

    for s in (0, 1):
        for c in part:
            ve.wait_ge(sem["m%d_%d" % (s, c)], 1)
            ve.tensor_copy(T["h%d" % (s + 1)][:, blk(own, c)], bank(s, c)[:, 0:wid(c)]).then_inc(a_sem(s + 1, own, c), 1)
    if not is_twin:
        for c in LAST:
            ve.wait_ge(sem["m2_%d" % c], 1)
            ve.tensor_copy(T.yo[:, BLK[c][0]:BLK[c][1]], bank(2, c)[:, 0:wid(c)]).then_inc(sem["f%d" % c], 1)
        qs = [g.sync, g.scalar]
        for n, c in enumerate(LAST):
            qs[n % 2].wait_ge(sem["f%d" % c], 1)
            qs[n % 2].dma_start(T.y[:, BLK[c][0]:BLK[c][1]], T.yo[:, BLK[c][0]:BLK[c][1]]).then_inc(sem["st%d" % c], 16)
        for n, c in enumerate(LAST):
            qs[n % 2].wait_ge(sem["st%d" % c], 16)
